import numpy as np
import ml_dtypes


def mxq(x, axis, fmt="e4m3"):
    dtype, down = {"e4m3": (ml_dtypes.float8_e4m3fn, 7), "e5m2": (ml_dtypes.float8_e5m2, 14)}[fmt]
    v = np.moveaxis(np.asarray(x, np.float32).astype(ml_dtypes.bfloat16).astype(np.float64), axis, -1)
    blocks = v.reshape(v.shape[:-1] + (-1, 32))
    amax = np.abs(blocks).max(-1, keepdims=True)
    byte = np.maximum(np.where(amax > 0, np.frexp(amax)[1] - 1 + 127, 0) - down, 1)
    scale = np.exp2(byte - 127.0)
    codes = (blocks / scale).astype(np.float32).astype(dtype).astype(np.float64)
    return np.moveaxis((codes * scale).reshape(v.shape), -1, axis)


WIDE = False


def mx_kscale(k):
    if not WIDE:
        return np.ones(k)
    levels = np.array([10, -10, 5, -5, 0])
    if k % 512:
        return np.exp2(np.random.permutation(np.resize(levels, k // 32))).repeat(32)
    a = np.empty((k // 512, 16))
    for p in range(k // 512):
        a[p, :8] = np.random.permutation(np.resize(levels, 8))
        for g in range(8):
            far = levels[np.abs(levels - a[p, g]) >= 10]
            a[p, g + 8] = far[np.random.randint(len(far))]
    return np.exp2(a.ravel()).repeat(32)


def f64(x):
    return np.asarray(x).astype(np.float64)


def striped(idx):
    return np.tile(idx.reshape(-1, 16).T, (8, 1)).astype(np.uint16)


def unstriped(offs):
    return offs[:16].T.reshape(-1).astype(np.int64)


E2M1 = np.array([0.0, 0.5, 1.0, 1.5, 2.0, 3.0, 4.0, 6.0, -0.0, -0.5, -1.0, -1.5, -2.0, -3.0, -4.0, -6.0])


def pack_weight(w, fmt):
    k, n = w.shape
    w = f64(np.asarray(w, np.float32).astype(ml_dtypes.bfloat16)).reshape(k // 32, 32, n)
    amax = np.abs(w).max(1)
    if fmt == "e4m3":
        byte = np.frexp(amax)[1] - 1 + 127 - 7
    else:
        mant, ex = np.frexp(amax / 6.0)
        byte = np.where(mant > 0.5, ex, ex - 1) + 127
    byte = np.clip(np.where(amax > 0, byte, 1), 1, 254)
    scaled = (w * np.exp2(127.0 - byte)[:, None, :]).reshape(k, n).astype(np.float32)
    by_word = np.ascontiguousarray(scaled.reshape(k // 512, 128, 4, n).transpose(0, 1, 3, 2))
    if fmt == "e4m3":
        words = by_word.astype(ml_dtypes.float8_e4m3fn).view(np.uint8)
    else:
        c = by_word.astype(ml_dtypes.float4_e2m1fn).view(np.uint8) & 0xF
        words = (c[..., 0::2] | (c[..., 1::2] << 4)).reshape(k // 512, 128, 2 * n)
    return np.ascontiguousarray(words), np.ascontiguousarray(byte.astype(np.uint8).reshape(k // 512, 16, n))


def unpack_weight(words, scales, fmt):
    g, _, n = scales.shape
    words = np.ascontiguousarray(words).reshape(g, 128, n, -1)
    if fmt == "e4m3":
        vals = words.view(ml_dtypes.float8_e4m3fn).astype(np.float64)
    else:
        nib = np.empty((g, 128, n, 4), np.uint8)
        nib[..., 0::2] = words & 0xF
        nib[..., 1::2] = words >> 4
        vals = E2M1[nib]
    vals = vals * np.repeat(np.exp2(scales.astype(np.float64) - 127.0), 8, axis=1)[..., None]
    return vals.transpose(0, 1, 3, 2).reshape(g * 512, n)


def gelu(v):
    return 0.5 * v * (1.0 + np.tanh(np.sqrt(2.0 / np.pi) * (v + 0.044715 * v**3)))


K, H, T, S, T2, P = 1024, 1024, 2048, 1024, 2048, 512

def setup_inputs():
    n = np.random.standard_normal
    s = mx_kscale(K)[:, None]
    u = mx_kscale(H)[:, None]
    tab_words, tab_scales = pack_weight(n((K, T)) * s, "e4m3")
    w2_words, w2_scales = pack_weight(0.8 * n((H, H)) / np.sqrt(H) / u * u.T, "e2m1")
    return {
        "tab_words": tab_words, "tab_scales": tab_scales,
        "offs": striped(np.random.permutation(T)[:S]),
        "offs2": striped(np.random.permutation(T2)[:S]),
        "offs3": striped(np.random.permutation(T2)[:P]),
        "offs4": striped(np.random.permutation(T2)[:P]),
        "w1": (n((K, H)) / np.sqrt(K) / s * u.T).astype(np.float32),
        "f1": np.exp(0.5 * n((H, S))).astype(np.float32),
        "wgs": np.exp(0.3 * n((128, S))).astype(np.float32),
        "page0": (n((H, T2)) * u).astype(np.float32),
        "b": (0.8 * n(H) * u[:, 0]).astype(np.float32),
        "f2": n((H, P)).astype(np.float32),
        "w2_words": w2_words, "w2_scales": w2_scales,
        "w3": (0.8 * n((H, H)) / np.sqrt(H) / u * u.T).astype(np.float32),
        "d": (0.7 * n(H) * u[:, 0]).astype(np.float32),
        "wgo": np.exp(0.3 * n((128, P))).astype(np.float32),
    }

def reference(tab_words, tab_scales, offs, offs2, offs3, offs4, w1, f1, wgs, page0, b, f2, w2_words, w2_scales, w3, d, wgo):
    v = unpack_weight(tab_words, tab_scales, "e4m3")[:, unstriped(offs)]
    h = (mxq(f64(w1), 0, "e4m3").T @ v) * f64(f1)
    page = f64(page0).copy()
    page[:, unstriped(offs2)] = np.tile(f64(wgs), (H // 128, 1)) * h
    x = page[:, unstriped(offs3)]
    xa = mxq(x + f64(b)[:, None], 0, "e4m3")
    xb = mxq(x * f64(f2), 0, "e4m3")
    w2 = unpack_weight(w2_words, w2_scales, "e2m1")
    w3q = mxq(f64(w3), 0, "e4m3")
    y = np.abs(w2.T @ xa + w3q.T @ xb) + f64(d)[:, None]
    page[:, unstriped(offs4)] = np.tile(f64(wgo), (H // 128, 1)) * y
    return page

@@ -1,0 +1,253 @@
+from contextlib import ExitStack
+
+import concourse.mybir as mybir
+
+K, H, T, S, T2, PM = 1024, 1024, 2048, 1024, 2048, 512
+FLOPS = 2 * K * H * S + 2 * 2 * H * H * PM
+
+F32 = mybir.dt.float32
+BF16 = mybir.dt.bfloat16
+I32 = mybir.dt.int32
+U32 = mybir.dt.uint32
+U16 = mybir.dt.uint16
+U8 = mybir.dt.uint8
+FP8X4 = mybir.dt.float8_e4m3fn_x4
+FP4X4 = mybir.dt.float4_e2m1fn_x4
+MULT = mybir.AluOpType.mult
+ACT = mybir.ActivationFunctionType
+
+P = 128
+PACK = 4
+KP = P * PACK
+NB = 512
+NTILES = H // P
+
+
+def tile_list_gas_ledger_rewrite_kernel(
+    tc, tab_words, tab_scales, offs, offs2, offs3, offs4, w1, f1, wgs, page0, b, f2, w2_words, w2_scales, w3, d, wgo, out
+):
+    nc = tc.nc
+    with ExitStack() as ctx:
+        keep = ctx.enter_context(tc.tile_pool(name="keep", bufs=1))
+        ring = ctx.enter_context(tc.tile_pool(name="ring", bufs=2))
+        psum = ctx.enter_context(tc.psum_pool(name="psum", bufs=4))
+
+        def rows_of(x, i):
+            return x.rearrange("(a p t) c -> a t p c", p=P, t=PACK)[i // PACK, i % PACK]
+
+        idx = keep.tile([P, S // 16], U16, name="idx")
+        idx2 = keep.tile([P, S // 16], U16, name="idx2")
+        idx3 = keep.tile([P, PM // 16], U16, name="idx3")
+        idx4 = keep.tile([P, PM // 16], U16, name="idx4")
+        tab_sc = keep.tile([P, T], U8, name="tab_sc", align_bytes=64)
+        w2_sc_raw = keep.tile([P, 2, H], U8, name="w2_sc_raw", align_bytes=64)
+        tab_w = [keep.tile([P, T], U32, name="tab_w%d" % a, tag="tab_w%d" % a, align_bytes=64) for a in range(2)]
+        v_w = [keep.tile([P, S], U32, name="v_w%d" % a, align_bytes=64) for a in range(2)]
+        v_sc = keep.tile([P, S], U8, name="v_sc", align_bytes=64)
+        page = [keep.tile([P, T2], F32, name="page%d" % i, align_bytes=64) for i in range(NTILES)]
+        wgs_sb = [keep.tile([P, S], F32, name="wgs%d" % t, align_bytes=64) for t in range(PACK)]
+        wgo_sb = keep.tile([P, PACK, PM], F32, name="wgo_sb", align_bytes=64)
+        b_sb = keep.tile([P, 2, PACK], F32, name="b_sb")
+        d_sb = keep.tile([P, 2, PACK], F32, name="d_sb")
+        w2_raw = keep.tile([P, 2, 2 * H], U8, name="w2_raw", align_bytes=64)
+
+        def load_weight(w, a, h):
+            raw = ring.tile([P, PACK, KP], F32, name="w_raw", align_bytes=64)
+            nc.sync.dma_start(out=raw[:], in_=w[KP * a : KP * (a + 1), KP * h : KP * (h + 1)].rearrange("(p j) c -> p j c", j=PACK))
+            return raw
+
+        def cast_into(grouped, raw):
+            nc.scalar.copy(out=grouped.rearrange("p t m j -> p m t j"), in_=raw[:].rearrange("p j (m t) -> p m t j", t=PACK))
+
+        def cast_weight(raw, slot):
+            grouped = keep.tile([P, PACK, P, PACK], BF16, name="w_bf", tag="sums_%d" % slot, align_bytes=64)
+            cast_into(grouped[:], raw)
+            return grouped
+
+        def quantize(src, width, name, scale_tag):
+            codes = keep.tile([P, width], U32, name=name + "_c", align_bytes=64)
+            scales = keep.tile([P, width], U8, name=name + "_s", tag=scale_tag, align_bytes=64)
+            nc.vector.quantize_mx(out=codes[:].bitcast(FP8X4), scales=scales[:], in_=src)
+            return codes, scales
+
+        def quantize_weight(grouped, name):
+            return quantize(grouped[:].rearrange("p t m j -> p (t m j)"), KP, name, name + "_s")
+
+        def load_wgs(t):
+            src = wgs.rearrange("(q t) j -> t q j", t=PACK)[t]
+            for q in range(4):
+                nc.sync.dma_start(out=wgs_sb[t][32 * q : 32 * (q + 1), :], in_=src)
+
+        f1_sb, f2_sb, x_sb, w1_q, w3_q = {}, {}, {}, {}, {}
+
+        def load_f1(i):
+            f1_sb[i] = keep.tile([P, S], F32, name="f1_%d" % i, tag="f1_%d" % (i % 4), align_bytes=64)
+            nc.sync.dma_start(out=f1_sb[i][:], in_=rows_of(f1, i))
+
+        def load_f2(i):
+            f2_sb[i] = keep.tile([P, PM], F32, name="f2_%d" % i, tag="f2_%d" % (i % 3), align_bytes=64)
+            nc.sync.dma_start(out=f2_sb[i][:], in_=rows_of(f2, i))
+
+        def load_page(i):
+            nc.sync.dma_start(out=page[i][:], in_=rows_of(page0, i))
+
+        def make_lines(i, pieces):
+            a_out, t = divmod(i, PACK)
+            sums = keep.tile([P, S], F32, name="sums", tag="sums_%d" % (i % 4), align_bytes=64)
+            for c in range(S // NB):
+                cols = slice(NB * c, NB * (c + 1))
+                acc = psum.tile([P, NB], F32, name="acc1", tag="acc1")
+                for a in range(2):
+                    codes, scales = w1_q[a, a_out]
+                    nc.tensor.matmul_mx(
+                        out=acc[:],
+                        lhsT=codes[:, P * t : P * (t + 1)].bitcast(FP8X4),
+                        lhsT_scale=scales[:, P * t : P * (t + 1)],
+                        rhs=v_w[a][:, cols].bitcast(FP8X4),
+                        rhs_scale=v_sc[4 * a : P, cols],
+                        start=(a == 0),
+                        stop=(a == 1),
+                    )
+                nc.scalar.copy(out=sums[:, cols], in_=acc[:])
+            for cols in pieces:
+                nc.gpsimd.tensor_tensor(f1_sb[i][:, cols], f1_sb[i][:, cols], wgs_sb[t][:, cols], MULT)
+                nc.gpsimd.tensor_tensor(f1_sb[i][:, cols], f1_sb[i][:, cols], sums[:, cols], MULT)
+
+        def put_lines(i, pieces):
+            for cols in pieces:
+                nc.vector.tensor_copy(page[i][:].indirect(idx2[:, cols.start // 16 : cols.stop // 16]), f1_sb[i][:, cols])
+
+        def fetch_lines(i):
+            x_sb[i] = keep.tile([P, PM], F32, name="x_%d" % i, tag="x_%d" % (i % 3), align_bytes=64)
+            nc.vector.tensor_copy(x_sb[i][:], page[i][:].indirect(idx3[:]))
+
+        def condition(i, woven):
+            a, t = divmod(i, PACK)
+            nc.scalar.activation(woven[:, 0, :, t], x_sb[i][:], ACT.Identity, bias=b_sb[:, a, t : t + 1])
+            nc.gpsimd.tensor_tensor(woven[:, 1, :, t], x_sb[i][:], f2_sb[i][:], MULT)
+
+        whole = [slice(0, S)]
+        halves = [slice(0, NB), slice(NB, S)]
+
+        nc.gpsimd.memset(tab_sc[:].bitcast(I32), 0)
+        nc.vector.memset(w2_sc_raw[:].rearrange("p a c -> p (a c)").bitcast(I32), 0)
+        nc.sync.dma_start(idx[:], offs)
+        for q in range(4):
+            nc.gpsimd.dma_start(out=tab_sc[32 * q : 32 * q + 8, :].bitcast(I32), in_=tab_scales[:, 4 * q : 4 * q + 4, :].bitcast(I32))
+        raw = {}
+        for a in range(2):
+            raw[a] = load_weight(w1, a, 0)
+            nc.sync.dma_start(out=tab_w[a][:].bitcast(I32), in_=tab_words[a].rearrange("p t i -> p (t i)").bitcast(I32))
+        nc.sync.dma_start(idx2[:], offs2)
+        load_f1(0)
+        load_wgs(0)
+        load_page(0)
+        nc.vector.tensor_copy(v_sc[:], tab_sc[:].indirect(idx[:]))
+        nc.vector.tensor_copy(v_w[0][:], tab_w[0][:].indirect(idx[:]))
+        w1_q[0, 0] = quantize_weight(cast_weight(raw[0], 2), "w1q00")
+        grouped = cast_weight(raw[1], 3)
+        nc.vector.tensor_copy(v_w[1][:, halves[0]], tab_w[1][:].indirect(idx[:, 0 : NB // 16]))
+        w1_q[1, 0] = quantize_weight(grouped, "w1q10")
+        nc.vector.tensor_copy(v_w[1][:, halves[1]], tab_w[1][:].indirect(idx[:, NB // 16 : S // 16]))
+        make_lines(0, halves)
+        load_f1(1)
+        load_wgs(1)
+        nc.sync.dma_start(idx3[:], offs3)
+        nc.sync.dma_start(out=b_sb[:], in_=b.rearrange("(a p t) -> p a t", p=P, t=PACK))
+        make_lines(1, whole)
+        w1_q[0, 1] = quantize_weight(cast_weight(load_weight(w1, 0, 1), 1), "w1q01")
+
+        woven = {}
+        x_q = {}
+        held = keep.tile([P, 2, PACK, P, PACK], BF16, name="held", tag="tab_w1", align_bytes=64)
+        for i in range(NTILES):
+            a, t = divmod(i, PACK)
+            if t == 0:
+                woven[a] = keep.tile([P, 2, PM, PACK], BF16, name="woven%d" % a, tag=("woven", "tab_w0")[a], align_bytes=64)
+            put_lines(i, halves if i == 0 else whole)
+            fetch_lines(i)
+            if i + 1 < NTILES:
+                load_page(i + 1)
+            if i < 5:
+                chunk = load_weight(*[(w1, 1, 1), (w3, 0, 0), (w3, 1, 0), (w3, 0, 1), (w3, 1, 1)][i])
+            if i + 2 < NTILES:
+                load_f1(i + 2)
+                if i + 2 < PACK:
+                    load_wgs(i + 2)
+            load_f2(i)
+            if i + 2 < NTILES:
+                make_lines(i + 2, whole)
+            if i == 0:
+                w1_q[1, 1] = quantize_weight(cast_weight(chunk, 2), "w1q11")
+            if i in (1, 2):
+                w3_q[i - 1, 0] = quantize_weight(cast_weight(chunk, (i + 2) % 4), "w3q%d0" % (i - 1))
+            if i in (3, 4):
+                cast_into(held[:, i - 3], chunk)
+            if i == 5:
+                nc.sync.dma_start(idx4[:], offs4)
+                nc.sync.dma_start(out=d_sb[:], in_=d.rearrange("(a p t) -> p a t", p=P, t=PACK))
+                for q in range(4):
+                    nc.sync.dma_start(out=wgo_sb[32 * q : 32 * (q + 1)], in_=wgo.rearrange("(q t) m -> q t m", t=PACK))
+            if i == 6:
+                nc.sync.dma_start(out=w2_raw[:].bitcast(I32), in_=w2_words.rearrange("a p c -> p a c").bitcast(I32))
+                for q in range(4):
+                    nc.sync.dma_start(
+                        out=w2_sc_raw[32 * q : 32 * q + 4].bitcast(I32),
+                        in_=w2_scales[:, 4 * q : 4 * q + 4, :].rearrange("a r c -> r a c").bitcast(I32),
+                    )
+            condition(i, woven[a])
+            if i == PACK - 1:
+                codes, scales = quantize(woven[0][:].rearrange("p s m t -> p (s m t)"), 2 * PM, "xq0", "xq0_s")
+                x_q[0, 0] = (codes[:, 0:PM], scales[:, 0:PM])
+                x_q[0, 1] = (codes[:, PM : 2 * PM], scales[:, PM : 2 * PM])
+
+        w2_w, w2_s = {}, {}
+
+        def deal_w2(h):
+            w2_w[h] = keep.tile([P, 2, 2 * KP], U8, name="w2_w%d" % h, align_bytes=64)
+            w2_s[h] = keep.tile([P, 2, KP], U8, name="w2_s%d" % h, align_bytes=64)
+            nc.vector.tensor_copy(
+                out=w2_w[h][:].bitcast(U16).rearrange("p a (t m) -> p a t m", t=PACK),
+                in_=w2_raw[:].bitcast(U16)[:, :, KP * h : KP * (h + 1)].rearrange("p a (m t) -> p a t m", t=PACK),
+            )
+            nc.vector.tensor_copy(
+                out=w2_s[h][:].rearrange("p a (t m) -> p a t m", t=PACK),
+                in_=w2_sc_raw[:, :, KP * h : KP * (h + 1)].rearrange("p a (m t) -> p a t m", t=PACK),
+            )
+
+        deal_w2(0)
+        for s in range(2):
+            codes, scales = quantize(woven[1][:, s].rearrange("p m t -> p (m t)"), PM, "xq1%d" % s, "xq1%d_s" % s)
+            x_q[1, s] = (codes[:], scales[:])
+        deal_w2(1)
+        codes, scales = quantize(held[:].rearrange("p a t m j -> p (a t m j)"), 2 * KP, "w3q1", "x_%d" % ((NTILES - 1) % 3))
+        for a in range(2):
+            w3_q[a, 1] = (codes[:, KP * a : KP * (a + 1)], scales[:, KP * a : KP * (a + 1)])
+
+        for i in range(NTILES):
+            h, t = divmod(i, PACK)
+            cols = slice(P * t, P * (t + 1))
+            acc = psum.tile([P, PM], F32, name="acc2", tag="acc2" if h == 0 else "acc1")
+            passes = [(1, 0), (0, 0), (0, 1), (1, 1)]
+            for n, (s, a) in enumerate(passes):
+                if s == 0:
+                    lhsT = w2_w[h][:, a, 2 * P * t : 2 * P * (t + 1)].bitcast(FP4X4)
+                    lhsT_scale = w2_s[h][:, a, cols]
+                else:
+                    lhsT = w3_q[a, h][0][:, cols].bitcast(FP8X4)
+                    lhsT_scale = w3_q[a, h][1][:, cols]
+                nc.tensor.matmul_mx(
+                    out=acc[:],
+                    lhsT=lhsT,
+                    lhsT_scale=lhsT_scale,
+                    rhs=x_q[a, s][0].bitcast(FP8X4),
+                    rhs_scale=x_q[a, s][1],
+                    start=(n == 0),
+                    stop=(n == len(passes) - 1),
+                )
+            magnitude = keep.tile([P, PM], F32, name="magnitude", tag="f1_%d" % (i % 2), align_bytes=64)
+            nc.scalar.activation(magnitude[:], acc[:], ACT.Abs)
+            y = keep.tile([P, PM], F32, name="y", tag="sums_%d" % (i % 4), align_bytes=64)
+            nc.scalar.activation(y[:], magnitude[:], ACT.Identity, bias=d_sb[:, h, t : t + 1])
+            nc.vector.tensor_tensor(page[i][:].indirect(idx4[:]), y[:], wgo_sb[:, t], MULT)
+            nc.sync.dma_start(out=rows_of(out, i), in_=page[i][:])

@@ -59,8 +59,8 @@ def tile_list_gas_ledger_rewrite_kernel(
         def cast_into(grouped, raw):
             nc.scalar.copy(out=grouped.rearrange("p t m j -> p m t j"), in_=raw[:].rearrange("p j (m t) -> p m t j", t=PACK))
 
-        def cast_weight(raw, slot):
-            grouped = keep.tile([P, PACK, P, PACK], BF16, name="w_bf", tag="sums_%d" % slot, align_bytes=64)
+        def cast_weight(raw):
+            grouped = ring.tile([P, PACK, P, PACK], BF16, name="w_bf", align_bytes=64)
             cast_into(grouped[:], raw)
             return grouped
 
@@ -73,16 +73,19 @@ def tile_list_gas_ledger_rewrite_kernel(
         def quantize_weight(grouped, name):
             return quantize(grouped[:].rearrange("p t m j -> p (t m j)"), KP, name, name + "_s")
 
-        def load_wgs(t):
+        def load_wgs(t, cols):
             src = wgs.rearrange("(q t) j -> t q j", t=PACK)[t]
             for q in range(4):
-                nc.sync.dma_start(out=wgs_sb[t][32 * q : 32 * (q + 1), :], in_=src)
+                nc.sync.dma_start(out=wgs_sb[t][32 * q : 32 * (q + 1), cols], in_=src[:, cols])
 
         f1_sb, f2_sb, x_sb, w1_q, w3_q = {}, {}, {}, {}, {}
 
-        def load_f1(i):
-            f1_sb[i] = keep.tile([P, S], F32, name="f1_%d" % i, tag="f1_%d" % (i % 4), align_bytes=64)
-            nc.sync.dma_start(out=f1_sb[i][:], in_=rows_of(f1, i))
+        def load_f1(i, cols):
+            if cols.start == 0:
+                f1_sb[i] = keep.tile([P, S], F32, name="f1_%d" % i, tag="f1_%d" % (i % 4), align_bytes=64)
+            nc.sync.dma_start(out=f1_sb[i][:, cols], in_=rows_of(f1, i)[:, cols])
+            if i < PACK:
+                load_wgs(i, cols)
 
         def load_f2(i):
             f2_sb[i] = keep.tile([P, PM], F32, name="f2_%d" % i, tag="f2_%d" % (i % 3), align_bytes=64)
@@ -91,11 +94,11 @@ def tile_list_gas_ledger_rewrite_kernel(
         def load_page(i):
             nc.sync.dma_start(out=page[i][:], in_=rows_of(page0, i))
 
-        def make_lines(i, pieces):
+        def make_lines(i):
             a_out, t = divmod(i, PACK)
-            sums = keep.tile([P, S], F32, name="sums", tag="sums_%d" % (i % 4), align_bytes=64)
-            for c in range(S // NB):
-                cols = slice(NB * c, NB * (c + 1))
+            for cols in halves if i == 0 else whole:
+                nc.gpsimd.tensor_tensor(f1_sb[i][:, cols], f1_sb[i][:, cols], wgs_sb[t][:, cols], MULT)
+            for c, cols in enumerate(halves):
                 acc = psum.tile([P, NB], F32, name="acc1", tag="acc1")
                 for a in range(2):
                     codes, scales = w1_q[a, a_out]
@@ -108,104 +111,47 @@ def tile_list_gas_ledger_rewrite_kernel(
                         start=(a == 0),
                         stop=(a == 1),
                     )
-                nc.scalar.copy(out=sums[:, cols], in_=acc[:])
-            for cols in pieces:
-                nc.gpsimd.tensor_tensor(f1_sb[i][:, cols], f1_sb[i][:, cols], wgs_sb[t][:, cols], MULT)
-                nc.gpsimd.tensor_tensor(f1_sb[i][:, cols], f1_sb[i][:, cols], sums[:, cols], MULT)
+                if (i, c) == (0, 0):
+                    nc.vector.tensor_tensor(f1_sb[i][:, cols], acc[:], f1_sb[i][:, cols], MULT)
+                else:
+                    tag = "sums_a%d" % (i % 4) if c == 0 else "sums_b%d" % (i % 6)
+                    sums = keep.tile([P, NB], F32, name="sums", tag=tag, align_bytes=64)
+                    nc.scalar.copy(out=sums[:], in_=acc[:])
+                    nc.gpsimd.tensor_tensor(f1_sb[i][:, cols], f1_sb[i][:, cols], sums[:], MULT)
 
-        def put_lines(i, pieces):
-            for cols in pieces:
+        def put_lines(i):
+            for cols in halves if i == 0 else whole:
                 nc.vector.tensor_copy(page[i][:].indirect(idx2[:, cols.start // 16 : cols.stop // 16]), f1_sb[i][:, cols])
 
+        def pieces_of_x(i):
+            return [slice(0, PM // 2), slice(PM // 2, PM)] if i == NTILES - 1 else [slice(0, PM)]
+
         def fetch_lines(i):
-            x_sb[i] = keep.tile([P, PM], F32, name="x_%d" % i, tag="x_%d" % (i % 3), align_bytes=64)
-            nc.vector.tensor_copy(x_sb[i][:], page[i][:].indirect(idx3[:]))
+            tag = {0: "x_free", 6: "x_free", 7: "sums_b1"}.get(i, "sums_b%d" % ((i + 1) % 6))
+            x_sb[i] = keep.tile([P, PM], F32, name="x_%d" % i, tag=tag, align_bytes=64)
+            for cols in pieces_of_x(i):
+                nc.vector.tensor_copy(x_sb[i][:, cols], page[i][:].indirect(idx3[:, cols.start // 16 : cols.stop // 16]))
 
-        def condition(i, woven):
+        def shift(i):
             a, t = divmod(i, PACK)
-            nc.scalar.activation(woven[:, 0, :, t], x_sb[i][:], ACT.Identity, bias=b_sb[:, a, t : t + 1])
-            nc.gpsimd.tensor_tensor(woven[:, 1, :, t], x_sb[i][:], f2_sb[i][:], MULT)
+            for cols in pieces_of_x(i):
+                nc.scalar.activation(woven[a][:, 0, cols, t], x_sb[i][:, cols], ACT.Identity, bias=b_sb[:, a, t : t + 1])
 
-        whole = [slice(0, S)]
-        halves = [slice(0, NB), slice(NB, S)]
-
-        nc.gpsimd.memset(tab_sc[:].bitcast(I32), 0)
-        nc.vector.memset(w2_sc_raw[:].rearrange("p a c -> p (a c)").bitcast(I32), 0)
-        nc.sync.dma_start(idx[:], offs)
-        for q in range(4):
-            nc.gpsimd.dma_start(out=tab_sc[32 * q : 32 * q + 8, :].bitcast(I32), in_=tab_scales[:, 4 * q : 4 * q + 4, :].bitcast(I32))
-        raw = {}
-        for a in range(2):
-            raw[a] = load_weight(w1, a, 0)
-            nc.sync.dma_start(out=tab_w[a][:].bitcast(I32), in_=tab_words[a].rearrange("p t i -> p (t i)").bitcast(I32))
-        nc.sync.dma_start(idx2[:], offs2)
-        load_f1(0)
-        load_wgs(0)
-        load_page(0)
-        nc.vector.tensor_copy(v_sc[:], tab_sc[:].indirect(idx[:]))
-        nc.vector.tensor_copy(v_w[0][:], tab_w[0][:].indirect(idx[:]))
-        w1_q[0, 0] = quantize_weight(cast_weight(raw[0], 2), "w1q00")
-        grouped = cast_weight(raw[1], 3)
-        nc.vector.tensor_copy(v_w[1][:, halves[0]], tab_w[1][:].indirect(idx[:, 0 : NB // 16]))
-        w1_q[1, 0] = quantize_weight(grouped, "w1q10")
-        nc.vector.tensor_copy(v_w[1][:, halves[1]], tab_w[1][:].indirect(idx[:, NB // 16 : S // 16]))
-        make_lines(0, halves)
-        load_f1(1)
-        load_wgs(1)
-        nc.sync.dma_start(idx3[:], offs3)
-        nc.sync.dma_start(out=b_sb[:], in_=b.rearrange("(a p t) -> p a t", p=P, t=PACK))
-        make_lines(1, whole)
-        w1_q[0, 1] = quantize_weight(cast_weight(load_weight(w1, 0, 1), 1), "w1q01")
-
-        woven = {}
-        x_q = {}
-        held = keep.tile([P, 2, PACK, P, PACK], BF16, name="held", tag="tab_w1", align_bytes=64)
-        for i in range(NTILES):
+        def condition(i):
             a, t = divmod(i, PACK)
-            if t == 0:
-                woven[a] = keep.tile([P, 2, PM, PACK], BF16, name="woven%d" % a, tag=("woven", "tab_w0")[a], align_bytes=64)
-            put_lines(i, halves if i == 0 else whole)
-            fetch_lines(i)
-            if i + 1 < NTILES:
-                load_page(i + 1)
-            if i < 5:
-                chunk = load_weight(*[(w1, 1, 1), (w3, 0, 0), (w3, 1, 0), (w3, 0, 1), (w3, 1, 1)][i])
-            if i + 2 < NTILES:
-                load_f1(i + 2)
-                if i + 2 < PACK:
-                    load_wgs(i + 2)
-            load_f2(i)
-            if i + 2 < NTILES:
-                make_lines(i + 2, whole)
-            if i == 0:
-                w1_q[1, 1] = quantize_weight(cast_weight(chunk, 2), "w1q11")
-            if i in (1, 2):
-                w3_q[i - 1, 0] = quantize_weight(cast_weight(chunk, (i + 2) % 4), "w3q%d0" % (i - 1))
-            if i in (3, 4):
-                cast_into(held[:, i - 3], chunk)
-            if i == 5:
-                nc.sync.dma_start(idx4[:], offs4)
-                nc.sync.dma_start(out=d_sb[:], in_=d.rearrange("(a p t) -> p a t", p=P, t=PACK))
-                for q in range(4):
-                    nc.sync.dma_start(out=wgo_sb[32 * q : 32 * (q + 1)], in_=wgo.rearrange("(q t) m -> q t m", t=PACK))
-            if i == 6:
-                nc.sync.dma_start(out=w2_raw[:].bitcast(I32), in_=w2_words.rearrange("a p c -> p a c").bitcast(I32))
-                for q in range(4):
-                    nc.sync.dma_start(
-                        out=w2_sc_raw[32 * q : 32 * q + 4].bitcast(I32),
-                        in_=w2_scales[:, 4 * q : 4 * q + 4, :].rearrange("a r c -> r a c").bitcast(I32),
-                    )
-            condition(i, woven[a])
-            if i == PACK - 1:
-                codes, scales = quantize(woven[0][:].rearrange("p s m t -> p (s m t)"), 2 * PM, "xq0", "xq0_s")
-                x_q[0, 0] = (codes[:, 0:PM], scales[:, 0:PM])
-                x_q[0, 1] = (codes[:, PM : 2 * PM], scales[:, PM : 2 * PM])
+            for cols in pieces_of_x(i):
+                nc.gpsimd.tensor_tensor(woven[a][:, 1, cols, t], x_sb[i][:, cols], f2_sb[i][:, cols], MULT)
+
+        def quantize_lines(a):
+            codes, scales = quantize(woven[a][:].rearrange("p s m t -> p (s m t)"), 2 * PM, "xq%d" % a, "xq%d_s" % a)
+            for s in range(2):
+                x_q[a, s] = (codes[:, PM * s : PM * (s + 1)], scales[:, PM * s : PM * (s + 1)])
 
         w2_w, w2_s = {}, {}
 
         def deal_w2(h):
-            w2_w[h] = keep.tile([P, 2, 2 * KP], U8, name="w2_w%d" % h, align_bytes=64)
-            w2_s[h] = keep.tile([P, 2, KP], U8, name="w2_s%d" % h, align_bytes=64)
+            w2_w[h] = keep.tile([P, 2, 2 * KP], U8, name="w2_w%d" % h, tag=("w2_w0", "tab_w0")[h], align_bytes=64)
+            w2_s[h] = keep.tile([P, 2, KP], U8, name="w2_s%d" % h, tag=("w2_s0", "f2_%d" % ((NTILES - 1) % 3))[h], align_bytes=64)
             nc.vector.tensor_copy(
                 out=w2_w[h][:].bitcast(U16).rearrange("p a (t m) -> p a t m", t=PACK),
                 in_=w2_raw[:].bitcast(U16)[:, :, KP * h : KP * (h + 1)].rearrange("p a (m t) -> p a t m", t=PACK),
@@ -215,12 +161,104 @@ def tile_list_gas_ledger_rewrite_kernel(
                 in_=w2_sc_raw[:, :, KP * h : KP * (h + 1)].rearrange("p a (m t) -> p a t m", t=PACK),
             )
 
-        deal_w2(0)
-        for s in range(2):
-            codes, scales = quantize(woven[1][:, s].rearrange("p m t -> p (m t)"), PM, "xq1%d" % s, "xq1%d_s" % s)
-            x_q[1, s] = (codes[:], scales[:])
+        whole = [slice(0, S)]
+        halves = [slice(0, NB), slice(NB, S)]
+
+        nc.gpsimd.memset(tab_sc[:].bitcast(I32), 0)
+        nc.vector.memset(w2_sc_raw[:].rearrange("p a c -> p (a c)").bitcast(I32), 0)
+        nc.sync.dma_start(idx[:], offs)
+        for q in range(4):
+            nc.scalar.dma_start(out=tab_sc[32 * q : 32 * q + 8, :].bitcast(I32), in_=tab_scales[:, 4 * q : 4 * q + 4, :].bitcast(I32))
+        raw = {}
+        for a in range(2):
+            raw[a] = load_weight(w1, a, 0)
+            nc.sync.dma_start(out=tab_w[a][:].bitcast(I32), in_=tab_words[a].rearrange("p t i -> p (t i)").bitcast(I32))
+        nc.sync.dma_start(idx2[:], offs2)
+        load_f1(0, halves[0])
+        load_page(0)
+        load_f1(0, halves[1])
+        nc.vector.tensor_copy(v_sc[:], tab_sc[:].indirect(idx[:]))
+        nc.vector.tensor_copy(v_w[0][:], tab_w[0][:].indirect(idx[:]))
+        w1_q[0, 0] = quantize_weight(cast_weight(raw[0]), "w1q00")
+        grouped = cast_weight(raw[1])
+        nc.vector.tensor_copy(v_w[1][:, halves[0]], tab_w[1][:].indirect(idx[:, 0 : NB // 16]))
+        w1_q[1, 0] = quantize_weight(grouped, "w1q10")
+        nc.vector.tensor_copy(v_w[1][:, halves[1]], tab_w[1][:].indirect(idx[:, NB // 16 : S // 16]))
+
+        woven = [
+            keep.tile([P, 2, PM, PACK], BF16, name="woven0", align_bytes=64),
+            keep.tile([P, 2, PM, PACK], BF16, name="woven1", tag="tab_w0", align_bytes=64),
+        ]
+        held = keep.tile([P, 2, PACK, P, PACK], BF16, name="held", tag="tab_w1", align_bytes=64)
+        x_q = {}
+
+        make_lines(0)
+        nc.sync.dma_start(idx3[:], offs3)
+        load_f1(1, whole[0])
+        load_page(1)
+        make_lines(1)
+        put_lines(0)
+        fetch_lines(0)
+        load_f1(2, whole[0])
+        make_lines(2)
+        put_lines(1)
+        w1_q[0, 1] = quantize_weight(cast_weight(load_weight(w1, 0, 1)), "w1q01")
+        load_page(2)
+        w1_q[1, 1] = quantize_weight(cast_weight(load_weight(w1, 1, 1)), "w1q11")
+        load_f1(3, whole[0])
+        make_lines(3)
+        load_page(3)
+        load_f2(0)
+        condition(0)
+        for i in range(1, NTILES - 1):
+            if i == NTILES - 2:
+                fetch_lines(i)
+            put_lines(i + 1)
+            if i < NTILES - 2:
+                fetch_lines(i)
+            if i + 3 < NTILES:
+                load_f1(i + 3, whole[0])
+                make_lines(i + 3)
+            if i in (1, 2):
+                w3_q[i - 1, 0] = quantize_weight(cast_weight(load_weight(w3, i - 1, 0)), "w3q%d0" % (i - 1))
+            if i in (3, 4):
+                cast_into(held[:, i - 3], load_weight(w3, i - 3, 1))
+            if i == 2:
+                nc.sync.dma_start(out=b_sb[:], in_=b.rearrange("(a p t) -> p a t", p=P, t=PACK))
+            if i != 3:
+                load_f2(i)
+            if i == 2:
+                load_f2(3)
+            if i + 3 < NTILES:
+                load_page(i + 3)
+            condition(i)
+            if i == 3:
+                for j in range(PACK):
+                    shift(j)
+                quantize_lines(0)
+            if i > 3:
+                shift(i)
+            if i == 3:
+                nc.sync.dma_start(out=w2_raw[:].bitcast(I32), in_=w2_words.rearrange("a p c -> p a c").bitcast(I32))
+                for q in range(4):
+                    nc.sync.dma_start(
+                        out=w2_sc_raw[32 * q : 32 * q + 4].bitcast(I32),
+                        in_=w2_scales[:, 4 * q : 4 * q + 4, :].rearrange("a r c -> r a c").bitcast(I32),
+                    )
+                deal_w2(0)
+            if i == 5:
+                nc.sync.dma_start(idx4[:], offs4)
+                nc.sync.dma_start(out=d_sb[:], in_=d.rearrange("(a p t) -> p a t", p=P, t=PACK))
+                for q in range(4):
+                    nc.sync.dma_start(out=wgo_sb[32 * q : 32 * (q + 1)], in_=wgo.rearrange("(q t) m -> q t m", t=PACK))
+        fetch_lines(NTILES - 1)
+        load_f2(NTILES - 1)
+        condition(NTILES - 1)
+        shift(NTILES - 1)
+
+        quantize_lines(1)
         deal_w2(1)
-        codes, scales = quantize(held[:].rearrange("p a t m j -> p (a t m j)"), 2 * KP, "w3q1", "x_%d" % ((NTILES - 1) % 3))
+        codes, scales = quantize(held[:].rearrange("p a t m j -> p (a t m j)"), 2 * KP, "w3q1", "sums_b1")
         for a in range(2):
             w3_q[a, 1] = (codes[:, KP * a : KP * (a + 1)], scales[:, KP * a : KP * (a + 1)])
 
@@ -247,7 +285,7 @@ def tile_list_gas_ledger_rewrite_kernel(
                 )
             magnitude = keep.tile([P, PM], F32, name="magnitude", tag="f1_%d" % (i % 2), align_bytes=64)
             nc.scalar.activation(magnitude[:], acc[:], ACT.Abs)
-            y = keep.tile([P, PM], F32, name="y", tag="sums_%d" % (i % 4), align_bytes=64)
+            y = keep.tile([P, PM], F32, name="y", tag="sums_a%d" % (i % 4), align_bytes=64)
             nc.scalar.activation(y[:], magnitude[:], ACT.Identity, bias=d_sb[:, h, t : t + 1])
             nc.vector.tensor_tensor(page[i][:].indirect(idx4[:]), y[:], wgo_sb[:, t], MULT)
             nc.sync.dma_start(out=rows_of(out, i), in_=page[i][:])

@@ -1,6 +1,7 @@
 from contextlib import ExitStack
 
 import concourse.mybir as mybir
+from concourse.masks import make_identity
 
 K, H, T, S, T2, PM = 1024, 1024, 2048, 1024, 2048, 512
 FLOPS = 2 * K * H * S + 2 * 2 * H * H * PM
@@ -46,7 +47,6 @@ def tile_list_gas_ledger_rewrite_kernel(
         v_sc = keep.tile([P, S], U8, name="v_sc", align_bytes=64)
         page = [keep.tile([P, T2], F32, name="page%d" % i, align_bytes=64) for i in range(NTILES)]
         wgs_sb = [keep.tile([P, S], F32, name="wgs%d" % t, align_bytes=64) for t in range(PACK)]
-        wgo_sb = keep.tile([P, PACK, PM], F32, name="wgo_sb", align_bytes=64)
         b_sb = keep.tile([P, 2, PACK], F32, name="b_sb")
         d_sb = keep.tile([P, 2, PACK], F32, name="d_sb")
         w2_raw = keep.tile([P, 2, 2 * H], U8, name="w2_raw", align_bytes=64)
@@ -73,19 +73,25 @@ def tile_list_gas_ledger_rewrite_kernel(
         def quantize_weight(grouped, name):
             return quantize(grouped[:].rearrange("p t m j -> p (t m j)"), KP, name, name + "_s")
 
-        def load_wgs(t, cols):
-            src = wgs.rearrange("(q t) j -> t q j", t=PACK)[t]
-            for q in range(4):
-                nc.sync.dma_start(out=wgs_sb[t][32 * q : 32 * (q + 1), cols], in_=src[:, cols])
+        def deal_wgs(t):
+            for k in range(2):
+                src = turned[k][:].rearrange("p b (q t) -> p b t q", t=PACK)[:, :, t, :]
+                nc.scalar.copy(
+                    out=spread[t // 2][:, t % 2, 4 * k : 4 * k + 4].rearrange("p b (u q) -> p b u q", u=4),
+                    in_=src.unsqueeze(2).to_broadcast([P, 4, 4, 32]),
+                )
+            for k in range(2):
+                back = psum.tile([P, 4, P], F32, name="back", tag="acc2")
+                for j in range(4):
+                    nc.tensor.transpose(back[:, j], spread[t // 2][:, t % 2, 4 * k + j], ident[:])
+                nc.scalar.copy(out=wgs_sb[t][:, NB * k : NB * (k + 1)], in_=back[:].rearrange("p b j -> p (b j)"))
 
-        f1_sb, f2_sb, x_sb, w1_q, w3_q = {}, {}, {}, {}, {}
+        f1_sb, f2_sb, x_sb, w1_q, w3_q, planes = {}, {}, {}, {}, {}, {}
 
         def load_f1(i, cols):
             if cols.start == 0:
                 f1_sb[i] = keep.tile([P, S], F32, name="f1_%d" % i, tag="f1_%d" % (i % 4), align_bytes=64)
             nc.sync.dma_start(out=f1_sb[i][:, cols], in_=rows_of(f1, i)[:, cols])
-            if i < PACK:
-                load_wgs(i, cols)
 
         def load_f2(i):
             f2_sb[i] = keep.tile([P, PM], F32, name="f2_%d" % i, tag="f2_%d" % (i % 3), align_bytes=64)
@@ -139,8 +145,15 @@ def tile_list_gas_ledger_rewrite_kernel(
 
         def condition(i):
             a, t = divmod(i, PACK)
+            if t == 0:
+                planes[a] = keep.tile([P, PACK, PM], BF16, name="planes%d" % a, tag="planes", align_bytes=64)
+            engine = nc.vector if i == NTILES - 1 else nc.gpsimd
             for cols in pieces_of_x(i):
-                nc.gpsimd.tensor_tensor(woven[a][:, 1, cols, t], x_sb[i][:, cols], f2_sb[i][:, cols], MULT)
+                engine.tensor_tensor(planes[a][:, t, cols], x_sb[i][:, cols], f2_sb[i][:, cols], MULT)
+
+        def weave(a):
+            copy = (nc.scalar.copy, nc.vector.tensor_copy)[a]
+            copy(woven[a][:, 1].rearrange("p (c i) t -> p c t i", i=4), planes[a][:].rearrange("p t (c i) -> p c t i", i=4))
 
         def quantize_lines(a):
             codes, scales = quantize(woven[a][:].rearrange("p s m t -> p (s m t)"), 2 * PM, "xq%d" % a, "xq%d_s" % a)
@@ -151,7 +164,7 @@ def tile_list_gas_ledger_rewrite_kernel(
 
         def deal_w2(h):
             w2_w[h] = keep.tile([P, 2, 2 * KP], U8, name="w2_w%d" % h, tag=("w2_w0", "tab_w0")[h], align_bytes=64)
-            w2_s[h] = keep.tile([P, 2, KP], U8, name="w2_s%d" % h, tag=("w2_s0", "f2_%d" % ((NTILES - 1) % 3))[h], align_bytes=64)
+            w2_s[h] = keep.tile([P, 2, KP], U8, name="w2_s%d" % h, tag=("w2_s0", "planes")[h], align_bytes=64)
             nc.vector.tensor_copy(
                 out=w2_w[h][:].bitcast(U16).rearrange("p a (t m) -> p a t m", t=PACK),
                 in_=w2_raw[:].bitcast(U16)[:, :, KP * h : KP * (h + 1)].rearrange("p a (m t) -> p a t m", t=PACK),
@@ -169,6 +182,15 @@ def tile_list_gas_ledger_rewrite_kernel(
         nc.sync.dma_start(idx[:], offs)
         for q in range(4):
             nc.scalar.dma_start(out=tab_sc[32 * q : 32 * q + 8, :].bitcast(I32), in_=tab_scales[:, 4 * q : 4 * q + 4, :].bitcast(I32))
+        ident = keep.tile([P, P], F32, name="ident", align_bytes=64)
+        make_identity(nc, ident[:])
+        wgs_rows = keep.tile([P, S], F32, name="wgs_rows", tag="f1_3", align_bytes=64)
+        nc.sync.dma_start(out=wgs_rows[:], in_=wgs)
+        turned = [psum.tile([P, 4, P], F32, name="turned%d" % k, tag="acc2") for k in range(2)]
+        for j in range(S // P):
+            nc.tensor.transpose(turned[j // 4][:, j % 4], wgs_rows[:, P * j : P * (j + 1)], ident[:])
+        spread = [keep.tile([P, 2, S // P, P], F32, name="spread%d" % n, tag=("woven0", "wgo_sb")[n], align_bytes=64) for n in range(2)]
+        deal_wgs(0)
         raw = {}
         for a in range(2):
             raw[a] = load_weight(w1, a, 0)
@@ -185,14 +207,17 @@ def tile_list_gas_ledger_rewrite_kernel(
         w1_q[1, 0] = quantize_weight(grouped, "w1q10")
         nc.vector.tensor_copy(v_w[1][:, halves[1]], tab_w[1][:].indirect(idx[:, NB // 16 : S // 16]))
 
-        woven = [
-            keep.tile([P, 2, PM, PACK], BF16, name="woven0", align_bytes=64),
-            keep.tile([P, 2, PM, PACK], BF16, name="woven1", tag="tab_w0", align_bytes=64),
-        ]
         held = keep.tile([P, 2, PACK, P, PACK], BF16, name="held", tag="tab_w1", align_bytes=64)
         x_q = {}
 
         make_lines(0)
+        for t in range(1, PACK):
+            deal_wgs(t)
+        wgo_sb = keep.tile([P, PACK, PM], F32, name="wgo_sb", tag="wgo_sb", align_bytes=64)
+        woven = [
+            keep.tile([P, 2, PM, PACK], BF16, name="woven0", tag="woven0", align_bytes=64),
+            keep.tile([P, 2, PM, PACK], BF16, name="woven1", tag="tab_w0", align_bytes=64),
+        ]
         nc.sync.dma_start(idx3[:], offs3)
         load_f1(1, whole[0])
         load_page(1)
@@ -235,6 +260,7 @@ def tile_list_gas_ledger_rewrite_kernel(
             if i == 3:
                 for j in range(PACK):
                     shift(j)
+                weave(0)
                 quantize_lines(0)
             if i > 3:
                 shift(i)
@@ -256,6 +282,7 @@ def tile_list_gas_ledger_rewrite_kernel(
         condition(NTILES - 1)
         shift(NTILES - 1)
 
+        weave(1)
         quantize_lines(1)
         deal_w2(1)
         codes, scales = quantize(held[:].rearrange("p a t m j -> p (a t m j)"), 2 * KP, "w3q1", "sums_b1")

@@ -70,6 +70,14 @@ def tile_list_gas_ledger_rewrite_kernel(
             nc.vector.quantize_mx(out=codes[:].bitcast(FP8X4), scales=scales[:], in_=src)
             return codes, scales
 
+        def pair_tile(name, tag):
+            return keep.tile([P, 2, PACK, P, PACK], BF16, name=name, tag=tag, align_bytes=64)
+
+        def quantize_pair(pair, into, h, name, scale_tag):
+            codes, scales = quantize(pair[:].rearrange("p a t m j -> p (a t m j)"), 2 * KP, name, scale_tag)
+            for a in range(2):
+                into[a, h] = (codes[:, KP * a : KP * (a + 1)], scales[:, KP * a : KP * (a + 1)])
+
         def quantize_weight(grouped, name):
             return quantize(grouped[:].rearrange("p t m j -> p (t m j)"), KP, name, name + "_s")
 
@@ -151,25 +159,27 @@ def tile_list_gas_ledger_rewrite_kernel(
             for cols in pieces_of_x(i):
                 engine.tensor_tensor(planes[a][:, t, cols], x_sb[i][:, cols], f2_sb[i][:, cols], MULT)
 
-        def weave(a):
+        def weave(a, cols):
             copy = (nc.scalar.copy, nc.vector.tensor_copy)[a]
-            copy(woven[a][:, 1].rearrange("p (c i) t -> p c t i", i=4), planes[a][:].rearrange("p t (c i) -> p c t i", i=4))
+            copy(woven[a][:, 1, cols].rearrange("p (c i) t -> p c t i", i=4), planes[a][:, :, cols].rearrange("p t (c i) -> p c t i", i=4))
 
-        def quantize_lines(a):
-            codes, scales = quantize(woven[a][:].rearrange("p s m t -> p (s m t)"), 2 * PM, "xq%d" % a, "xq%d_s" % a)
-            for s in range(2):
-                x_q[a, s] = (codes[:, PM * s : PM * (s + 1)], scales[:, PM * s : PM * (s + 1)])
+        def quantize_lines(a, s, cols):
+            codes, scales = x_q[a, s]
+            nc.vector.quantize_mx(
+                out=codes[:, cols].bitcast(FP8X4), scales=scales[:, cols], in_=woven[a][:, s, cols].rearrange("p m t -> p (m t)")
+            )
 
         w2_w, w2_s = {}, {}
 
         def deal_w2(h):
-            w2_w[h] = keep.tile([P, 2, 2 * KP], U8, name="w2_w%d" % h, tag=("w2_w0", "tab_w0")[h], align_bytes=64)
-            w2_s[h] = keep.tile([P, 2, KP], U8, name="w2_s%d" % h, tag=("w2_s0", "planes")[h], align_bytes=64)
-            nc.vector.tensor_copy(
-                out=w2_w[h][:].bitcast(U16).rearrange("p a (t m) -> p a t m", t=PACK),
-                in_=w2_raw[:].bitcast(U16)[:, :, KP * h : KP * (h + 1)].rearrange("p a (m t) -> p a t m", t=PACK),
-            )
-            nc.vector.tensor_copy(
+            w2_w[h] = keep.tile([P, 2, 2 * KP], U8, name="w2_w%d" % h, align_bytes=64)
+            w2_s[h] = keep.tile([P, 2, KP], U8, name="w2_s%d" % h, align_bytes=64)
+            for a in range(2):
+                nc.gpsimd.tensor_copy(
+                    out=w2_w[h][:, a].rearrange("p (t m e) -> p t m e", t=PACK, e=2),
+                    in_=w2_raw[:, a, 2 * KP * h : 2 * KP * (h + 1)].rearrange("p (m t e) -> p t m e", t=PACK, e=2),
+                )
+            nc.gpsimd.tensor_copy(
                 out=w2_s[h][:].rearrange("p a (t m) -> p a t m", t=PACK),
                 in_=w2_sc_raw[:, :, KP * h : KP * (h + 1)].rearrange("p a (m t) -> p a t m", t=PACK),
             )
@@ -207,17 +217,13 @@ def tile_list_gas_ledger_rewrite_kernel(
         w1_q[1, 0] = quantize_weight(grouped, "w1q10")
         nc.vector.tensor_copy(v_w[1][:, halves[1]], tab_w[1][:].indirect(idx[:, NB // 16 : S // 16]))
 
-        held = keep.tile([P, 2, PACK, P, PACK], BF16, name="held", tag="tab_w1", align_bytes=64)
         x_q = {}
 
         make_lines(0)
         for t in range(1, PACK):
             deal_wgs(t)
         wgo_sb = keep.tile([P, PACK, PM], F32, name="wgo_sb", tag="wgo_sb", align_bytes=64)
-        woven = [
-            keep.tile([P, 2, PM, PACK], BF16, name="woven0", tag="woven0", align_bytes=64),
-            keep.tile([P, 2, PM, PACK], BF16, name="woven1", tag="tab_w0", align_bytes=64),
-        ]
+        woven = {0: keep.tile([P, 2, PM, PACK], BF16, name="woven0", tag="woven0", align_bytes=64)}
         nc.sync.dma_start(idx3[:], offs3)
         load_f1(1, whole[0])
         load_page(1)
@@ -227,25 +233,43 @@ def tile_list_gas_ledger_rewrite_kernel(
         load_f1(2, whole[0])
         make_lines(2)
         put_lines(1)
-        w1_q[0, 1] = quantize_weight(cast_weight(load_weight(w1, 0, 1)), "w1q01")
+        pair = pair_tile("w1_pair", "tab_w1")
+        cast_into(pair[:, 0], load_weight(w1, 0, 1))
         load_page(2)
-        w1_q[1, 1] = quantize_weight(cast_weight(load_weight(w1, 1, 1)), "w1q11")
+        cast_into(pair[:, 1], load_weight(w1, 1, 1))
+        quantize_pair(pair, w1_q, 1, "w1q1", "w1q1_s")
         load_f1(3, whole[0])
         make_lines(3)
         load_page(3)
         load_f2(0)
+        nc.sync.dma_start(out=w2_raw[:].bitcast(I32), in_=w2_words.rearrange("a p c -> p a c").bitcast(I32))
+        for q in range(4):
+            nc.sync.dma_start(
+                out=w2_sc_raw[32 * q : 32 * q + 4].bitcast(I32),
+                in_=w2_scales[:, 4 * q : 4 * q + 4, :].rearrange("a r c -> r a c").bitcast(I32),
+            )
         condition(0)
+        deal_w2(0)
+        pair = pair_tile("w3_pair", "tab_w0")
+        held = pair_tile("held", "tab_w1")
         for i in range(1, NTILES - 1):
             if i == NTILES - 2:
                 fetch_lines(i)
             put_lines(i + 1)
+            if i == 5:
+                codes, scales = quantize(woven[0][:].rearrange("p s m t -> p (s m t)"), 2 * PM, "xq0", "f1_2")
+                for s in range(2):
+                    x_q[0, s] = (codes[:, PM * s : PM * (s + 1)], scales[:, PM * s : PM * (s + 1)])
             if i < NTILES - 2:
                 fetch_lines(i)
             if i + 3 < NTILES:
                 load_f1(i + 3, whole[0])
                 make_lines(i + 3)
             if i in (1, 2):
-                w3_q[i - 1, 0] = quantize_weight(cast_weight(load_weight(w3, i - 1, 0)), "w3q%d0" % (i - 1))
+                cast_into(pair[:, i - 1], load_weight(w3, i - 1, 0))
+            if i == 2:
+                quantize_pair(pair, w3_q, 0, "w3q0", "w3q0_s")
+                woven[1] = keep.tile([P, 2, PM, PACK], BF16, name="woven1", tag="tab_w0", align_bytes=64)
             if i in (3, 4):
                 cast_into(held[:, i - 3], load_weight(w3, i - 3, 1))
             if i == 2:
@@ -257,21 +281,14 @@ def tile_list_gas_ledger_rewrite_kernel(
             if i + 3 < NTILES:
                 load_page(i + 3)
             condition(i)
+            if i == 2:
+                deal_w2(1)
             if i == 3:
                 for j in range(PACK):
                     shift(j)
-                weave(0)
-                quantize_lines(0)
+                weave(0, slice(0, PM))
             if i > 3:
                 shift(i)
-            if i == 3:
-                nc.sync.dma_start(out=w2_raw[:].bitcast(I32), in_=w2_words.rearrange("a p c -> p a c").bitcast(I32))
-                for q in range(4):
-                    nc.sync.dma_start(
-                        out=w2_sc_raw[32 * q : 32 * q + 4].bitcast(I32),
-                        in_=w2_scales[:, 4 * q : 4 * q + 4, :].rearrange("a r c -> r a c").bitcast(I32),
-                    )
-                deal_w2(0)
             if i == 5:
                 nc.sync.dma_start(idx4[:], offs4)
                 nc.sync.dma_start(out=d_sb[:], in_=d.rearrange("(a p t) -> p a t", p=P, t=PACK))
@@ -282,19 +299,26 @@ def tile_list_gas_ledger_rewrite_kernel(
         condition(NTILES - 1)
         shift(NTILES - 1)
 
-        weave(1)
-        quantize_lines(1)
-        deal_w2(1)
-        codes, scales = quantize(held[:].rearrange("p a t m j -> p (a t m j)"), 2 * KP, "w3q1", "sums_b1")
-        for a in range(2):
-            w3_q[a, 1] = (codes[:, KP * a : KP * (a + 1)], scales[:, KP * a : KP * (a + 1)])
+        for s in range(2):
+            x_q[1, s] = (
+                keep.tile([P, PM], U32, name="xq1%d_c" % s, align_bytes=64),
+                keep.tile([P, PM], U8, name="xq1%d_s" % s, align_bytes=64),
+            )
+        first, second = pieces_of_x(NTILES - 1)
+        for cols in (first, second):
+            weave(1, cols)
+            quantize_lines(1, 0, cols)
+            quantize_lines(1, 1, cols)
+        quantize_pair(held, w3_q, 1, "w3q1", "sums_b1")
 
-        for i in range(NTILES):
+        steps = [(0, first), (0, second)] + [(i, slice(0, PM)) for i in range(1, NTILES)]
+        for n, (i, lines) in enumerate(steps):
             h, t = divmod(i, PACK)
             cols = slice(P * t, P * (t + 1))
-            acc = psum.tile([P, PM], F32, name="acc2", tag="acc2" if h == 0 else "acc1")
+            width = lines.stop - lines.start
+            acc = psum.tile([P, width], F32, name="acc2", tag=("acc2", "acc1")[n // 4 % 2])
             passes = [(1, 0), (0, 0), (0, 1), (1, 1)]
-            for n, (s, a) in enumerate(passes):
+            for k, (s, a) in enumerate(passes):
                 if s == 0:
                     lhsT = w2_w[h][:, a, 2 * P * t : 2 * P * (t + 1)].bitcast(FP4X4)
                     lhsT_scale = w2_s[h][:, a, cols]
@@ -305,14 +329,15 @@ def tile_list_gas_ledger_rewrite_kernel(
                     out=acc[:],
                     lhsT=lhsT,
                     lhsT_scale=lhsT_scale,
-                    rhs=x_q[a, s][0].bitcast(FP8X4),
-                    rhs_scale=x_q[a, s][1],
-                    start=(n == 0),
-                    stop=(n == len(passes) - 1),
+                    rhs=x_q[a, s][0][:, lines].bitcast(FP8X4),
+                    rhs_scale=x_q[a, s][1][:, lines],
+                    start=(k == 0),
+                    stop=(k == len(passes) - 1),
                 )
-            magnitude = keep.tile([P, PM], F32, name="magnitude", tag="f1_%d" % (i % 2), align_bytes=64)
+            magnitude = keep.tile([P, width], F32, name="magnitude", tag="f1_%d" % (n % 2), align_bytes=64)
             nc.scalar.activation(magnitude[:], acc[:], ACT.Abs)
-            y = keep.tile([P, PM], F32, name="y", tag="sums_a%d" % (i % 4), align_bytes=64)
+            y = keep.tile([P, width], F32, name="y", tag="sums_a%d" % (n % 4), align_bytes=64)
             nc.scalar.activation(y[:], magnitude[:], ACT.Identity, bias=d_sb[:, h, t : t + 1])
-            nc.vector.tensor_tensor(page[i][:].indirect(idx4[:]), y[:], wgo_sb[:, t], MULT)
-            nc.sync.dma_start(out=rows_of(out, i), in_=page[i][:])
+            nc.vector.tensor_tensor(page[i][:].indirect(idx4[:, lines.start // 16 : lines.stop // 16]), y[:], wgo_sb[:, t, lines], MULT)
+            if lines.stop == PM:
+                nc.sync.dma_start(out=rows_of(out, i), in_=page[i][:])

@@ -102,7 +102,7 @@ def tile_list_gas_ledger_rewrite_kernel(
             nc.sync.dma_start(out=f1_sb[i][:, cols], in_=rows_of(f1, i)[:, cols])
 
         def load_f2(i):
-            f2_sb[i] = keep.tile([P, PM], F32, name="f2_%d" % i, tag="f2_%d" % (i % 3), align_bytes=64)
+            f2_sb[i] = keep.tile([P, PM], F32, name="f2_%d" % i, tag="f2_%d" % (i % 4), align_bytes=64)
             nc.sync.dma_start(out=f2_sb[i][:], in_=rows_of(f2, i))
 
         def load_page(i):
@@ -110,9 +110,11 @@ def tile_list_gas_ledger_rewrite_kernel(
 
         def make_lines(i):
             a_out, t = divmod(i, PACK)
-            for cols in halves if i == 0 else whole:
-                nc.gpsimd.tensor_tensor(f1_sb[i][:, cols], f1_sb[i][:, cols], wgs_sb[t][:, cols], MULT)
+            if i >= 2:
+                nc.gpsimd.tensor_tensor(f1_sb[i][:], f1_sb[i][:], wgs_sb[t][:], MULT)
             for c, cols in enumerate(halves):
+                if i < 2:
+                    nc.gpsimd.tensor_tensor(f1_sb[i][:, cols], f1_sb[i][:, cols], wgs_sb[t][:, cols], MULT)
                 acc = psum.tile([P, NB], F32, name="acc1", tag="acc1")
                 for a in range(2):
                     codes, scales = w1_q[a, a_out]
@@ -128,14 +130,13 @@ def tile_list_gas_ledger_rewrite_kernel(
                 if (i, c) == (0, 0):
                     nc.vector.tensor_tensor(f1_sb[i][:, cols], acc[:], f1_sb[i][:, cols], MULT)
                 else:
-                    tag = "sums_a%d" % (i % 4) if c == 0 else "sums_b%d" % (i % 6)
+                    tag = "x_free" if (i, c) == (1, 0) else "sums_a%d" % (i % 4) if c == 0 else "sums_b%d" % (i % 6)
                     sums = keep.tile([P, NB], F32, name="sums", tag=tag, align_bytes=64)
                     nc.scalar.copy(out=sums[:], in_=acc[:])
                     nc.gpsimd.tensor_tensor(f1_sb[i][:, cols], f1_sb[i][:, cols], sums[:], MULT)
 
-        def put_lines(i):
-            for cols in halves if i == 0 else whole:
-                nc.vector.tensor_copy(page[i][:].indirect(idx2[:, cols.start // 16 : cols.stop // 16]), f1_sb[i][:, cols])
+        def put_lines(i, cols):
+            nc.vector.tensor_copy(page[i][:].indirect(idx2[:, cols.start // 16 : cols.stop // 16]), f1_sb[i][:, cols])
 
         def pieces_of_x(i):
             return [slice(0, PM // 2), slice(PM // 2, PM)] if i == NTILES - 1 else [slice(0, PM)]
@@ -169,19 +170,13 @@ def tile_list_gas_ledger_rewrite_kernel(
                 out=codes[:, cols].bitcast(FP8X4), scales=scales[:, cols], in_=woven[a][:, s, cols].rearrange("p m t -> p (m t)")
             )
 
-        w2_w, w2_s = {}, {}
+        w2_w = {}
 
-        def deal_w2(h):
-            w2_w[h] = keep.tile([P, 2, 2 * KP], U8, name="w2_w%d" % h, align_bytes=64)
-            w2_s[h] = keep.tile([P, 2, KP], U8, name="w2_s%d" % h, align_bytes=64)
-            for a in range(2):
-                nc.gpsimd.tensor_copy(
-                    out=w2_w[h][:, a].rearrange("p (t m e) -> p t m e", t=PACK, e=2),
-                    in_=w2_raw[:, a, 2 * KP * h : 2 * KP * (h + 1)].rearrange("p (m t e) -> p t m e", t=PACK, e=2),
-                )
-            nc.gpsimd.tensor_copy(
-                out=w2_s[h][:].rearrange("p a (t m) -> p a t m", t=PACK),
-                in_=w2_sc_raw[:, :, KP * h : KP * (h + 1)].rearrange("p a (m t) -> p a t m", t=PACK),
+        def deal_w2_words(h):
+            w2_w[h] = keep.tile([P, 2, 2 * KP], U8, name="w2_w%d" % h, tag=("woven0", "tab_w0")[h], align_bytes=64)
+            nc.vector.tensor_copy(
+                out=w2_w[h][:].bitcast(U16).rearrange("p a (t m) -> p a t m", t=PACK),
+                in_=w2_raw[:].bitcast(U16)[:, :, KP * h : KP * (h + 1)].rearrange("p a (m t) -> p a t m", t=PACK),
             )
 
         whole = [slice(0, S)]
@@ -220,46 +215,48 @@ def tile_list_gas_ledger_rewrite_kernel(
         x_q = {}
 
         make_lines(0)
-        for t in range(1, PACK):
-            deal_wgs(t)
-        wgo_sb = keep.tile([P, PACK, PM], F32, name="wgo_sb", tag="wgo_sb", align_bytes=64)
-        woven = {0: keep.tile([P, 2, PM, PACK], BF16, name="woven0", tag="woven0", align_bytes=64)}
+        deal_wgs(1)
         nc.sync.dma_start(idx3[:], offs3)
         load_f1(1, whole[0])
         load_page(1)
         make_lines(1)
-        put_lines(0)
+        put_lines(0, halves[0])
+        put_lines(0, halves[1])
+        put_lines(1, halves[0])
         fetch_lines(0)
+        put_lines(1, halves[1])
         load_f1(2, whole[0])
+        deal_wgs(2)
         make_lines(2)
-        put_lines(1)
         pair = pair_tile("w1_pair", "tab_w1")
         cast_into(pair[:, 0], load_weight(w1, 0, 1))
         load_page(2)
         cast_into(pair[:, 1], load_weight(w1, 1, 1))
         quantize_pair(pair, w1_q, 1, "w1q1", "w1q1_s")
         load_f1(3, whole[0])
+        deal_wgs(3)
+        wgo_sb = keep.tile([P, PACK, PM], F32, name="wgo_sb", tag="wgo_sb", align_bytes=64)
+        woven = {0: keep.tile([P, 2, PM, PACK], BF16, name="woven0", tag="woven0", align_bytes=64)}
         make_lines(3)
         load_page(3)
         load_f2(0)
-        nc.sync.dma_start(out=w2_raw[:].bitcast(I32), in_=w2_words.rearrange("a p c -> p a c").bitcast(I32))
-        for q in range(4):
-            nc.sync.dma_start(
-                out=w2_sc_raw[32 * q : 32 * q + 4].bitcast(I32),
-                in_=w2_scales[:, 4 * q : 4 * q + 4, :].rearrange("a r c -> r a c").bitcast(I32),
-            )
         condition(0)
-        deal_w2(0)
         pair = pair_tile("w3_pair", "tab_w0")
         held = pair_tile("held", "tab_w1")
         for i in range(1, NTILES - 1):
             if i == NTILES - 2:
                 fetch_lines(i)
-            put_lines(i + 1)
+            put_lines(i + 1, whole[0])
             if i == 5:
-                codes, scales = quantize(woven[0][:].rearrange("p s m t -> p (s m t)"), 2 * PM, "xq0", "f1_2")
-                for s in range(2):
-                    x_q[0, s] = (codes[:, PM * s : PM * (s + 1)], scales[:, PM * s : PM * (s + 1)])
+                both = keep.tile([P, 2, 2 * KP], U8, name="both", tag="f1_2", align_bytes=64)
+                for n, (src, into) in enumerate(((pair[:].rearrange("p a t m j -> p (a t m j)"), w3_q), (woven[0][:].rearrange("p s m t -> p (s m t)"), x_q))):
+                    codes = keep.tile([P, 2 * KP], U32, name="mid%d_c" % n, align_bytes=64)
+                    nc.vector.quantize_mx(out=codes[:].bitcast(FP8X4), scales=both[:, n], in_=src)
+                    for k in range(2):
+                        into[(k, 0) if n == 0 else (0, k)] = (codes[:, KP * k : KP * (k + 1)], both[:, n, KP * k : KP * (k + 1)])
+                deal_w2_words(0)
+                woven[1] = keep.tile([P, 2, PM, PACK], BF16, name="woven1", tag="tab_w0", align_bytes=64)
+                shift(4)
             if i < NTILES - 2:
                 fetch_lines(i)
             if i + 3 < NTILES:
@@ -267,35 +264,40 @@ def tile_list_gas_ledger_rewrite_kernel(
                 make_lines(i + 3)
             if i in (1, 2):
                 cast_into(pair[:, i - 1], load_weight(w3, i - 1, 0))
-            if i == 2:
-                quantize_pair(pair, w3_q, 0, "w3q0", "w3q0_s")
-                woven[1] = keep.tile([P, 2, PM, PACK], BF16, name="woven1", tag="tab_w0", align_bytes=64)
             if i in (3, 4):
                 cast_into(held[:, i - 3], load_weight(w3, i - 3, 1))
             if i == 2:
                 nc.sync.dma_start(out=b_sb[:], in_=b.rearrange("(a p t) -> p a t", p=P, t=PACK))
-            if i != 3:
-                load_f2(i)
-            if i == 2:
-                load_f2(3)
+            for j in {1: [1], 2: [2, 3], 4: [4, 5], 5: [6, 7]}.get(i, []):
+                load_f2(j)
             if i + 3 < NTILES:
                 load_page(i + 3)
             condition(i)
-            if i == 2:
-                deal_w2(1)
             if i == 3:
                 for j in range(PACK):
                     shift(j)
                 weave(0, slice(0, PM))
-            if i > 3:
+            if i > 4:
                 shift(i)
+            if i == 4:
+                nc.sync.dma_start(out=w2_raw[:].bitcast(I32), in_=w2_words.rearrange("a p c -> p a c").bitcast(I32))
+                for q in range(4):
+                    nc.sync.dma_start(
+                        out=w2_sc_raw[32 * q : 32 * q + 4].bitcast(I32),
+                        in_=w2_scales[:, 4 * q : 4 * q + 4, :].rearrange("a r c -> r a c").bitcast(I32),
+                    )
             if i == 5:
                 nc.sync.dma_start(idx4[:], offs4)
                 nc.sync.dma_start(out=d_sb[:], in_=d.rearrange("(a p t) -> p a t", p=P, t=PACK))
                 for q in range(4):
                     nc.sync.dma_start(out=wgo_sb[32 * q : 32 * (q + 1)], in_=wgo.rearrange("(q t) m -> q t m", t=PACK))
+        w2_s = keep.tile([P, 2, 2, KP], U8, name="w2_s", tag="f2_2", align_bytes=64)
+        for h in range(2):
+            nc.gpsimd.tensor_copy(
+                out=w2_s[:, :, h].rearrange("p a (t m) -> p a t m", t=PACK),
+                in_=w2_sc_raw[:, :, KP * h : KP * (h + 1)].rearrange("p a (m t) -> p a t m", t=PACK),
+            )
         fetch_lines(NTILES - 1)
-        load_f2(NTILES - 1)
         condition(NTILES - 1)
         shift(NTILES - 1)
 
@@ -310,6 +312,7 @@ def tile_list_gas_ledger_rewrite_kernel(
             quantize_lines(1, 0, cols)
             quantize_lines(1, 1, cols)
         quantize_pair(held, w3_q, 1, "w3q1", "sums_b1")
+        deal_w2_words(1)
 
         steps = [(0, first), (0, second)] + [(i, slice(0, PM)) for i in range(1, NTILES)]
         for n, (i, lines) in enumerate(steps):
@@ -321,7 +324,7 @@ def tile_list_gas_ledger_rewrite_kernel(
             for k, (s, a) in enumerate(passes):
                 if s == 0:
                     lhsT = w2_w[h][:, a, 2 * P * t : 2 * P * (t + 1)].bitcast(FP4X4)
-                    lhsT_scale = w2_s[h][:, a, cols]
+                    lhsT_scale = w2_s[:, a, h, cols]
                 else:
                     lhsT = w3_q[a, h][0][:, cols].bitcast(FP8X4)
                     lhsT_scale = w3_q[a, h][1][:, cols]

from contextlib import ExitStack

import concourse.mybir as mybir
from concourse.masks import make_identity

K, H, T, S, T2, PM = 1024, 1024, 2048, 1024, 2048, 512
FLOPS = 2 * K * H * S + 2 * 2 * H * H * PM

F32 = mybir.dt.float32
BF16 = mybir.dt.bfloat16
I32 = mybir.dt.int32
U32 = mybir.dt.uint32
U16 = mybir.dt.uint16
U8 = mybir.dt.uint8
FP8X4 = mybir.dt.float8_e4m3fn_x4
FP4X4 = mybir.dt.float4_e2m1fn_x4
MULT = mybir.AluOpType.mult
ACT = mybir.ActivationFunctionType

P = 128
PACK = 4
KP = P * PACK
NB = 512
NTILES = H // P


def tile_list_gas_ledger_rewrite_kernel(
    tc, tab_words, tab_scales, offs, offs2, offs3, offs4, w1, f1, wgs, page0, b, f2, w2_words, w2_scales, w3, d, wgo, out
):
    nc = tc.nc
    with ExitStack() as ctx:
        keep = ctx.enter_context(tc.tile_pool(name="keep", bufs=1))
        ring = ctx.enter_context(tc.tile_pool(name="ring", bufs=2))
        psum = ctx.enter_context(tc.psum_pool(name="psum", bufs=4))

        def rows_of(x, i):
            return x.rearrange("(a p t) c -> a t p c", p=P, t=PACK)[i // PACK, i % PACK]

        idx = keep.tile([P, S // 16], U16, name="idx")
        idx2 = keep.tile([P, S // 16], U16, name="idx2")
        idx3 = keep.tile([P, PM // 16], U16, name="idx3")
        idx4 = keep.tile([P, PM // 16], U16, name="idx4")
        tab_sc = keep.tile([P, T], U8, name="tab_sc", align_bytes=64)
        w2_sc_raw = keep.tile([P, 2, H], U8, name="w2_sc_raw", align_bytes=64)
        tab_w = [keep.tile([P, T], U32, name="tab_w%d" % a, tag="tab_w%d" % a, align_bytes=64) for a in range(2)]
        v_w = [keep.tile([P, S], U32, name="v_w%d" % a, align_bytes=64) for a in range(2)]
        v_sc = keep.tile([P, S], U8, name="v_sc", align_bytes=64)
        page = [keep.tile([P, T2], F32, name="page%d" % i, align_bytes=64) for i in range(NTILES)]
        wgs_sb = [keep.tile([P, S], F32, name="wgs%d" % t, align_bytes=64) for t in range(PACK)]
        b_sb = keep.tile([P, 2, PACK], F32, name="b_sb")
        d_sb = keep.tile([P, 2, PACK], F32, name="d_sb")
        w2_raw = keep.tile([P, 2, 2 * H], U8, name="w2_raw", align_bytes=64)

        def load_weight(w, a, h):
            raw = ring.tile([P, PACK, KP], F32, name="w_raw", align_bytes=64)
            nc.sync.dma_start(out=raw[:], in_=w[KP * a : KP * (a + 1), KP * h : KP * (h + 1)].rearrange("(p j) c -> p j c", j=PACK))
            return raw

        def cast_into(grouped, raw):
            nc.scalar.copy(out=grouped.rearrange("p t m j -> p m t j"), in_=raw[:].rearrange("p j (m t) -> p m t j", t=PACK))

        def cast_weight(raw):
            grouped = ring.tile([P, PACK, P, PACK], BF16, name="w_bf", align_bytes=64)
            cast_into(grouped[:], raw)
            return grouped

        def quantize(src, width, name, scale_tag):
            codes = keep.tile([P, width], U32, name=name + "_c", align_bytes=64)
            scales = keep.tile([P, width], U8, name=name + "_s", tag=scale_tag, align_bytes=64)
            nc.vector.quantize_mx(out=codes[:].bitcast(FP8X4), scales=scales[:], in_=src)
            return codes, scales

        def pair_tile(name, tag):
            return keep.tile([P, 2, PACK, P, PACK], BF16, name=name, tag=tag, align_bytes=64)

        def quantize_pair(pair, into, h, name, scale_tag):
            codes, scales = quantize(pair[:].rearrange("p a t m j -> p (a t m j)"), 2 * KP, name, scale_tag)
            for a in range(2):
                into[a, h] = (codes[:, KP * a : KP * (a + 1)], scales[:, KP * a : KP * (a + 1)])

        def quantize_weight(grouped, name):
            return quantize(grouped[:].rearrange("p t m j -> p (t m j)"), KP, name, name + "_s")

        def deal_wgs(t):
            for k in range(2):
                src = turned[k][:].rearrange("p b (q t) -> p b t q", t=PACK)[:, :, t, :]
                nc.scalar.copy(
                    out=spread[t // 2][:, t % 2, 4 * k : 4 * k + 4].rearrange("p b (u q) -> p b u q", u=4),
                    in_=src.unsqueeze(2).to_broadcast([P, 4, 4, 32]),
                )
            for k in range(2):
                back = psum.tile([P, 4, P], F32, name="back", tag="acc2")
                for j in range(4):
                    nc.tensor.transpose(back[:, j], spread[t // 2][:, t % 2, 4 * k + j], ident[:])
                nc.scalar.copy(out=wgs_sb[t][:, NB * k : NB * (k + 1)], in_=back[:].rearrange("p b j -> p (b j)"))

        f1_sb, f2_sb, x_sb, w1_q, w3_q, planes = {}, {}, {}, {}, {}, {}

        def load_f1(i, cols):
            if cols.start == 0:
                f1_sb[i] = keep.tile([P, S], F32, name="f1_%d" % i, tag="f1_%d" % (i % 4), align_bytes=64)
            nc.sync.dma_start(out=f1_sb[i][:, cols], in_=rows_of(f1, i)[:, cols])

        def load_f2(i):
            f2_sb[i] = keep.tile([P, PM], F32, name="f2_%d" % i, tag="f2_%d" % (i % 4), align_bytes=64)
            nc.sync.dma_start(out=f2_sb[i][:], in_=rows_of(f2, i))

        def load_page(i):
            nc.sync.dma_start(out=page[i][:], in_=rows_of(page0, i))

        def make_lines(i):
            a_out, t = divmod(i, PACK)
            if i >= 2:
                nc.gpsimd.tensor_tensor(f1_sb[i][:], f1_sb[i][:], wgs_sb[t][:], MULT)
            for c, cols in enumerate(halves):
                if i < 2:
                    nc.gpsimd.tensor_tensor(f1_sb[i][:, cols], f1_sb[i][:, cols], wgs_sb[t][:, cols], MULT)
                acc = psum.tile([P, NB], F32, name="acc1", tag="acc1")
                for a in range(2):
                    codes, scales = w1_q[a, a_out]
                    nc.tensor.matmul_mx(
                        out=acc[:],
                        lhsT=codes[:, P * t : P * (t + 1)].bitcast(FP8X4),
                        lhsT_scale=scales[:, P * t : P * (t + 1)],
                        rhs=v_w[a][:, cols].bitcast(FP8X4),
                        rhs_scale=v_sc[4 * a : P, cols],
                        start=(a == 0),
                        stop=(a == 1),
                    )
                if (i, c) == (0, 0):
                    nc.vector.tensor_tensor(f1_sb[i][:, cols], acc[:], f1_sb[i][:, cols], MULT)
                else:
                    tag = "x_free" if (i, c) == (1, 0) else "sums_a%d" % (i % 4) if c == 0 else "sums_b%d" % (i % 6)
                    sums = keep.tile([P, NB], F32, name="sums", tag=tag, align_bytes=64)
                    nc.scalar.copy(out=sums[:], in_=acc[:])
                    nc.gpsimd.tensor_tensor(f1_sb[i][:, cols], f1_sb[i][:, cols], sums[:], MULT)

        def put_lines(i, cols):
            nc.vector.tensor_copy(page[i][:].indirect(idx2[:, cols.start // 16 : cols.stop // 16]), f1_sb[i][:, cols])

        def pieces_of_x(i):
            return [slice(0, PM // 2), slice(PM // 2, PM)] if i == NTILES - 1 else [slice(0, PM)]

        def fetch_lines(i):
            tag = {0: "x_free", 6: "x_free", 7: "sums_b1"}.get(i, "sums_b%d" % ((i + 1) % 6))
            x_sb[i] = keep.tile([P, PM], F32, name="x_%d" % i, tag=tag, align_bytes=64)
            for cols in pieces_of_x(i):
                nc.vector.tensor_copy(x_sb[i][:, cols], page[i][:].indirect(idx3[:, cols.start // 16 : cols.stop // 16]))

        def shift(i):
            a, t = divmod(i, PACK)
            for cols in pieces_of_x(i):
                nc.scalar.activation(woven[a][:, 0, cols, t], x_sb[i][:, cols], ACT.Identity, bias=b_sb[:, a, t : t + 1])

        def condition(i):
            a, t = divmod(i, PACK)
            if t == 0:
                planes[a] = keep.tile([P, PACK, PM], BF16, name="planes%d" % a, tag="planes", align_bytes=64)
            engine = nc.vector if i == NTILES - 1 else nc.gpsimd
            for cols in pieces_of_x(i):
                engine.tensor_tensor(planes[a][:, t, cols], x_sb[i][:, cols], f2_sb[i][:, cols], MULT)

        def weave(a, cols):
            copy = (nc.scalar.copy, nc.vector.tensor_copy)[a]
            copy(woven[a][:, 1, cols].rearrange("p (c i) t -> p c t i", i=4), planes[a][:, :, cols].rearrange("p t (c i) -> p c t i", i=4))

        def quantize_lines(a, s, cols):
            codes, scales = x_q[a, s]
            nc.vector.quantize_mx(
                out=codes[:, cols].bitcast(FP8X4), scales=scales[:, cols], in_=woven[a][:, s, cols].rearrange("p m t -> p (m t)")
            )

        w2_w = {}

        def deal_w2_words(h):
            w2_w[h] = keep.tile([P, 2, 2 * KP], U8, name="w2_w%d" % h, tag=("woven0", "tab_w0")[h], align_bytes=64)
            nc.vector.tensor_copy(
                out=w2_w[h][:].bitcast(U16).rearrange("p a (t m) -> p a t m", t=PACK),
                in_=w2_raw[:].bitcast(U16)[:, :, KP * h : KP * (h + 1)].rearrange("p a (m t) -> p a t m", t=PACK),
            )

        whole = [slice(0, S)]
        halves = [slice(0, NB), slice(NB, S)]

        nc.gpsimd.memset(tab_sc[:].bitcast(I32), 0)
        nc.vector.memset(w2_sc_raw[:].rearrange("p a c -> p (a c)").bitcast(I32), 0)
        nc.sync.dma_start(idx[:], offs)
        for q in range(4):
            nc.scalar.dma_start(out=tab_sc[32 * q : 32 * q + 8, :].bitcast(I32), in_=tab_scales[:, 4 * q : 4 * q + 4, :].bitcast(I32))
        ident = keep.tile([P, P], F32, name="ident", align_bytes=64)
        make_identity(nc, ident[:])
        wgs_rows = keep.tile([P, S], F32, name="wgs_rows", tag="f1_3", align_bytes=64)
        nc.sync.dma_start(out=wgs_rows[:], in_=wgs)
        turned = [psum.tile([P, 4, P], F32, name="turned%d" % k, tag="acc2") for k in range(2)]
        for j in range(S // P):
            nc.tensor.transpose(turned[j // 4][:, j % 4], wgs_rows[:, P * j : P * (j + 1)], ident[:])
        spread = [keep.tile([P, 2, S // P, P], F32, name="spread%d" % n, tag=("woven0", "wgo_sb")[n], align_bytes=64) for n in range(2)]
        deal_wgs(0)
        raw = {}
        for a in range(2):
            raw[a] = load_weight(w1, a, 0)
            nc.sync.dma_start(out=tab_w[a][:].bitcast(I32), in_=tab_words[a].rearrange("p t i -> p (t i)").bitcast(I32))
        nc.sync.dma_start(idx2[:], offs2)
        load_f1(0, halves[0])
        load_page(0)
        load_f1(0, halves[1])
        nc.vector.tensor_copy(v_sc[:], tab_sc[:].indirect(idx[:]))
        nc.vector.tensor_copy(v_w[0][:], tab_w[0][:].indirect(idx[:]))
        w1_q[0, 0] = quantize_weight(cast_weight(raw[0]), "w1q00")
        grouped = cast_weight(raw[1])
        nc.vector.tensor_copy(v_w[1][:, halves[0]], tab_w[1][:].indirect(idx[:, 0 : NB // 16]))
        w1_q[1, 0] = quantize_weight(grouped, "w1q10")
        nc.vector.tensor_copy(v_w[1][:, halves[1]], tab_w[1][:].indirect(idx[:, NB // 16 : S // 16]))

        x_q = {}

        make_lines(0)
        deal_wgs(1)
        nc.sync.dma_start(idx3[:], offs3)
        load_f1(1, whole[0])
        load_page(1)
        make_lines(1)
        put_lines(0, halves[0])
        put_lines(0, halves[1])
        put_lines(1, halves[0])
        fetch_lines(0)
        put_lines(1, halves[1])
        load_f1(2, whole[0])
        deal_wgs(2)
        make_lines(2)
        pair = pair_tile("w1_pair", "tab_w1")
        cast_into(pair[:, 0], load_weight(w1, 0, 1))
        load_page(2)
        cast_into(pair[:, 1], load_weight(w1, 1, 1))
        quantize_pair(pair, w1_q, 1, "w1q1", "w1q1_s")
        load_f1(3, whole[0])
        deal_wgs(3)
        wgo_sb = keep.tile([P, PACK, PM], F32, name="wgo_sb", tag="wgo_sb", align_bytes=64)
        woven = {0: keep.tile([P, 2, PM, PACK], BF16, name="woven0", tag="woven0", align_bytes=64)}
        make_lines(3)
        load_page(3)
        load_f2(0)
        condition(0)
        pair = pair_tile("w3_pair", "tab_w0")
        held = pair_tile("held", "tab_w1")
        for i in range(1, NTILES - 1):
            if i == NTILES - 2:
                fetch_lines(i)
            put_lines(i + 1, whole[0])
            if i == 5:
                both = keep.tile([P, 2, 2 * KP], U8, name="both", tag="f1_2", align_bytes=64)
                for n, (src, into) in enumerate(((pair[:].rearrange("p a t m j -> p (a t m j)"), w3_q), (woven[0][:].rearrange("p s m t -> p (s m t)"), x_q))):
                    codes = keep.tile([P, 2 * KP], U32, name="mid%d_c" % n, align_bytes=64)
                    nc.vector.quantize_mx(out=codes[:].bitcast(FP8X4), scales=both[:, n], in_=src)
                    for k in range(2):
                        into[(k, 0) if n == 0 else (0, k)] = (codes[:, KP * k : KP * (k + 1)], both[:, n, KP * k : KP * (k + 1)])
                deal_w2_words(0)
                woven[1] = keep.tile([P, 2, PM, PACK], BF16, name="woven1", tag="tab_w0", align_bytes=64)
                shift(4)
            if i < NTILES - 2:
                fetch_lines(i)
            if i + 3 < NTILES:
                load_f1(i + 3, whole[0])
                make_lines(i + 3)
            if i in (1, 2):
                cast_into(pair[:, i - 1], load_weight(w3, i - 1, 0))
            if i in (3, 4):
                cast_into(held[:, i - 3], load_weight(w3, i - 3, 1))
            if i == 2:
                nc.sync.dma_start(out=b_sb[:], in_=b.rearrange("(a p t) -> p a t", p=P, t=PACK))
            for j in {1: [1], 2: [2, 3], 4: [4, 5], 5: [6, 7]}.get(i, []):
                load_f2(j)
            if i + 3 < NTILES:
                load_page(i + 3)
            condition(i)
            if i == 3:
                for j in range(PACK):
                    shift(j)
                weave(0, slice(0, PM))
            if i > 4:
                shift(i)
            if i == 4:
                nc.sync.dma_start(out=w2_raw[:].bitcast(I32), in_=w2_words.rearrange("a p c -> p a c").bitcast(I32))
                for q in range(4):
                    nc.sync.dma_start(
                        out=w2_sc_raw[32 * q : 32 * q + 4].bitcast(I32),
                        in_=w2_scales[:, 4 * q : 4 * q + 4, :].rearrange("a r c -> r a c").bitcast(I32),
                    )
            if i == 5:
                nc.sync.dma_start(idx4[:], offs4)
                nc.sync.dma_start(out=d_sb[:], in_=d.rearrange("(a p t) -> p a t", p=P, t=PACK))
                for q in range(4):
                    nc.sync.dma_start(out=wgo_sb[32 * q : 32 * (q + 1)], in_=wgo.rearrange("(q t) m -> q t m", t=PACK))
        w2_s = keep.tile([P, 2, 2, KP], U8, name="w2_s", tag="f2_2", align_bytes=64)
        for h in range(2):
            nc.gpsimd.tensor_copy(
                out=w2_s[:, :, h].rearrange("p a (t m) -> p a t m", t=PACK),
                in_=w2_sc_raw[:, :, KP * h : KP * (h + 1)].rearrange("p a (m t) -> p a t m", t=PACK),
            )
        fetch_lines(NTILES - 1)
        condition(NTILES - 1)
        shift(NTILES - 1)

        for s in range(2):
            x_q[1, s] = (
                keep.tile([P, PM], U32, name="xq1%d_c" % s, align_bytes=64),
                keep.tile([P, PM], U8, name="xq1%d_s" % s, align_bytes=64),
            )
        first, second = pieces_of_x(NTILES - 1)
        for cols in (first, second):
            weave(1, cols)
            quantize_lines(1, 0, cols)
            quantize_lines(1, 1, cols)
        quantize_pair(held, w3_q, 1, "w3q1", "sums_b1")
        deal_w2_words(1)

        steps = [(0, first), (0, second)] + [(i, slice(0, PM)) for i in range(1, NTILES)]
        for n, (i, lines) in enumerate(steps):
            h, t = divmod(i, PACK)
            cols = slice(P * t, P * (t + 1))
            width = lines.stop - lines.start
            acc = psum.tile([P, width], F32, name="acc2", tag=("acc2", "acc1")[n // 4 % 2])
            passes = [(1, 0), (0, 0), (0, 1), (1, 1)]
            for k, (s, a) in enumerate(passes):
                if s == 0:
                    lhsT = w2_w[h][:, a, 2 * P * t : 2 * P * (t + 1)].bitcast(FP4X4)
                    lhsT_scale = w2_s[:, a, h, cols]
                else:
                    lhsT = w3_q[a, h][0][:, cols].bitcast(FP8X4)
                    lhsT_scale = w3_q[a, h][1][:, cols]
                nc.tensor.matmul_mx(
                    out=acc[:],
                    lhsT=lhsT,
                    lhsT_scale=lhsT_scale,
                    rhs=x_q[a, s][0][:, lines].bitcast(FP8X4),
                    rhs_scale=x_q[a, s][1][:, lines],
                    start=(k == 0),
                    stop=(k == len(passes) - 1),
                )
            magnitude = keep.tile([P, width], F32, name="magnitude", tag="f1_%d" % (n % 2), align_bytes=64)
            nc.scalar.activation(magnitude[:], acc[:], ACT.Abs)
            y = keep.tile([P, width], F32, name="y", tag="sums_a%d" % (n % 4), align_bytes=64)
            nc.scalar.activation(y[:], magnitude[:], ACT.Identity, bias=d_sb[:, h, t : t + 1])
            nc.vector.tensor_tensor(page[i][:].indirect(idx4[:, lines.start // 16 : lines.stop // 16]), y[:], wgo_sb[:, t, lines], MULT)
            if lines.stop == PM:
                nc.sync.dma_start(out=rows_of(out, i), in_=page[i][:])
